import numpy as np
import ml_dtypes


def mxq(x, axis, fmt="e4m3"):
    dtype, down = {"e4m3": (ml_dtypes.float8_e4m3fn, 7), "e5m2": (ml_dtypes.float8_e5m2, 14)}[fmt]
    v = np.moveaxis(np.asarray(x, np.float32).astype(ml_dtypes.bfloat16).astype(np.float64), axis, -1)
    blocks = v.reshape(v.shape[:-1] + (-1, 32))
    amax = np.abs(blocks).max(-1, keepdims=True)
    byte = np.maximum(np.where(amax > 0, np.frexp(amax)[1] - 1 + 127, 0) - down, 1)
    scale = np.exp2(byte - 127.0)
    codes = (blocks / scale).astype(np.float32).astype(dtype).astype(np.float64)
    return np.moveaxis((codes * scale).reshape(v.shape), -1, axis)


WIDE = False


def mx_kscale(k):
    if not WIDE:
        return np.ones(k)
    levels = np.array([10, -10, 5, -5, 0])
    if k % 512:
        return np.exp2(np.random.permutation(np.resize(levels, k // 32))).repeat(32)
    a = np.empty((k // 512, 16))
    for p in range(k // 512):
        a[p, :8] = np.random.permutation(np.resize(levels, 8))
        for g in range(8):
            far = levels[np.abs(levels - a[p, g]) >= 10]
            a[p, g + 8] = far[np.random.randint(len(far))]
    return np.exp2(a.ravel()).repeat(32)


def f64(x):
    return np.asarray(x).astype(np.float64)


def striped(idx):
    return np.tile(np.asarray(idx).reshape(-1, 16).T, (8, 1)).astype(np.uint16)


def unstriped(offs):
    return offs[:16].T.reshape(-1).astype(np.int64)


E2M1 = np.array([0.0, 0.5, 1.0, 1.5, 2.0, 3.0, 4.0, 6.0, -0.0, -0.5, -1.0, -1.5, -2.0, -3.0, -4.0, -6.0])


def pack_weight(w, fmt):
    k, n = w.shape
    w = f64(np.asarray(w, np.float32).astype(ml_dtypes.bfloat16)).reshape(k // 32, 32, n)
    amax = np.abs(w).max(1)
    if fmt == "e4m3":
        byte = np.frexp(amax)[1] - 1 + 127 - 7
    else:
        mant, ex = np.frexp(amax / 6.0)
        byte = np.where(mant > 0.5, ex, ex - 1) + 127
    byte = np.clip(np.where(amax > 0, byte, 1), 1, 254)
    scaled = (w * np.exp2(127.0 - byte)[:, None, :]).reshape(k, n).astype(np.float32)
    by_word = np.ascontiguousarray(scaled.reshape(k // 512, 128, 4, n).transpose(0, 1, 3, 2))
    if fmt == "e4m3":
        words = by_word.astype(ml_dtypes.float8_e4m3fn).view(np.uint8)
    else:
        c = by_word.astype(ml_dtypes.float4_e2m1fn).view(np.uint8) & 0xF
        words = (c[..., 0::2] | (c[..., 1::2] << 4)).reshape(k // 512, 128, 2 * n)
    return np.ascontiguousarray(words), np.ascontiguousarray(byte.astype(np.uint8).reshape(k // 512, 16, n))


def unpack_weight(words, scales, fmt):
    g, _, n = scales.shape
    words = np.ascontiguousarray(words).reshape(g, 128, n, -1)
    if fmt == "e4m3":
        vals = words.view(ml_dtypes.float8_e4m3fn).astype(np.float64)
    else:
        nib = np.empty((g, 128, n, 4), np.uint8)
        nib[..., 0::2] = words & 0xF
        nib[..., 1::2] = words >> 4
        vals = E2M1[nib]
    vals = vals * np.repeat(np.exp2(scales.astype(np.float64) - 127.0), 8, axis=1)[..., None]
    return vals.transpose(0, 1, 3, 2).reshape(g * 512, n)


def bf(x):
    return np.asarray(x, np.float32).astype(ml_dtypes.bfloat16)


def planes(Y):
    r, m = Y.shape
    b = f64(bf(Y)).reshape(r // 32, 32, m)
    amax = np.abs(b).max(1)
    byte = np.clip(np.where(amax > 0, np.frexp(amax)[1] - 1 + 127 - 7, 1), 1, 254)
    codes = (b * np.exp2(127.0 - byte)[:, None, :]).reshape(r, m).astype(np.float32).astype(ml_dtypes.float8_e4m3fn).view(np.uint8)
    words = codes.reshape(r // 512, 128, 4, m).transpose(0, 1, 3, 2)
    return np.ascontiguousarray(words), np.ascontiguousarray(byte.astype(np.uint8).reshape(r // 512, 16, m))


D, E, T, I, Q = 512, 512, 2048, 512, 256


def setup_inputs():
    n = np.random.standard_normal
    idx2 = np.random.permutation(I)[:I]
    idx = np.random.permutation(T)[:I]
    fd = mx_kscale(D)
    fi = mx_kscale(I)
    ti = np.ones(T)
    ti[idx] = fi
    keysp = pack_weight(n((D, T)) / fd[:, None], "e4m3")
    return {
        "query": (n((D, Q)) * 0.8 / np.sqrt(D) * fd[:, None]).astype(np.float32),
        "keys_words": keysp[0],
        "keys_scales": keysp[1],
        "reserve": (np.random.uniform(0.5, 2.0, (Q, 1))).astype(np.float32),
        "os": (np.random.uniform(4.0, 16.0, (1, I)) * fi).astype(np.float32),
        "vals": (n((E, T)) / ti).astype(np.float32),
        "offs2": striped(idx2),
        "offs": striped(idx),
    }


def reference(query, keys_words, keys_scales, reserve, os, vals, offs2, offs):
    idx2 = unstriped(offs2)
    idx = unstriped(offs)
    keysu = unpack_weight(keys_words, keys_scales, "e4m3")
    queryq = mxq(f64(query), 0, "e4m3")
    keysidxg = keysu[:, idx]
    a = queryq.T @ keysidxg
    p = np.exp(a)
    z = np.sum(p, axis=1, keepdims=True)
    r = p / (p + p[:, idx2] + f64(reserve))
    w = p / z * r
    wo1 = w * f64(os)
    wt1 = wo1.T
    vt1 = f64(vals)[:, idx].T
    vt1q = mxq(vt1, 0, "e4m3")
    wt1q = mxq(wt1, 0, "e4m3")
    o = vt1q.T @ wt1q
    words, scales = planes(o)
    return o, words, scales

@@ -1,0 +1,231 @@
+from contextlib import ExitStack
+
+import concourse.mybir as mybir
+from concourse.masks import make_identity
+
+D, E, T, I, Q = 512, 512, 2048, 512, 256
+FLOPS = 2 * D * Q * I + 2 * I * E * Q
+
+F32 = mybir.dt.float32
+BF16 = mybir.dt.bfloat16
+U32 = mybir.dt.uint32
+I32 = mybir.dt.int32
+U16 = mybir.dt.uint16
+U8 = mybir.dt.uint8
+FP8X4 = mybir.dt.float8_e4m3fn_x4
+ALU = mybir.AluOpType
+ACT = mybir.ActivationFunctionType
+AX = mybir.AxisListType
+
+P = 128
+PACK = 4
+HALVES = Q // P
+SPARE = 16
+BIG = 1e30
+TINY = 1e-30
+
+
+def tile_attend_neighbourshare_pl_kernel(
+    tc, query, keys_words, keys_scales, reserve, slot_factor, vals, offs2, offs, out_0, out_1, out_2
+):
+    nc = tc.nc
+    with ExitStack() as ctx:
+        keep = ctx.enter_context(tc.tile_pool(name="keep", bufs=1))
+        psum = ctx.enter_context(tc.psum_pool(name="psum", bufs=1))
+        psum2 = ctx.enter_context(tc.psum_pool(name="psum2", bufs=2))
+
+        def sb(name, shape, dtype):
+            return keep.tile(shape, dtype, name=name, align_bytes=64)
+
+        offs_sb = sb("offs_sb", [P, I // 16], U16)
+        offs2_sb = sb("offs2_sb", [P, I // 16], U16)
+        kw_pool = sb("kw_pool", [P, T], I32)
+        ks_pool = sb("ks_pool", [P, T], U8)
+        nc.vector.memset(ks_pool[:].bitcast(I32), 0)
+        nc.sync.dma_start(offs_sb[:], offs)
+        for quad in range(4):
+            nc.scalar.dma_start(
+                ks_pool[32 * quad : 32 * quad + 4, :].bitcast(I32),
+                keys_scales[0, 4 * quad : 4 * quad + 4, :].bitcast(I32),
+            )
+        nc.sync.dma_start(kw_pool[:], keys_words[0].rearrange("p n t -> p (n t)").bitcast(I32))
+        q_view = query.rearrange("(p j) q -> p j q", j=PACK)
+        q_raw = []
+        for h in range(HALVES):
+            t = sb("q_raw%d" % h, [P, PACK, P], F32)
+            nc.sync.dma_start(t[:], q_view[:, :, h * P : (h + 1) * P])
+            q_raw.append(t)
+        v_view = vals.rearrange("(p j) t -> p j t", j=PACK)
+        v_pool = [sb("v_pool%d" % j, [P, T], F32) for j in range(PACK)]
+        nc.sync.dma_start(v_pool[0][:], v_view[:, 0, :])
+        nc.sync.dma_start(offs2_sb[:], offs2)
+        os_col = sb("os_col", [P, PACK], F32)
+        nc.sync.dma_start(os_col[:], slot_factor.rearrange("o (s r) -> s (o r)", r=PACK))
+        res = []
+        for h in range(HALVES):
+            t = sb("res%d" % h, [P, 1], F32)
+            nc.sync.dma_start(t[:], reserve[h * P : (h + 1) * P, :])
+            res.append(t)
+        for j in range(1, PACK):
+            nc.sync.dma_start(v_pool[j][:], v_view[:, j, :])
+
+        ident = sb("ident", [P, P], F32)
+        make_identity(nc, ident[:])
+
+        ks = sb("ks", [P, I], U8)
+        nc.vector.tensor_copy(ks[:], ks_pool[:].indirect(offs_sb[:]))
+        kw = sb("kw", [P, I], U32)
+        nc.vector.tensor_copy(kw[:], kw_pool[:].bitcast(U32).indirect(offs_sb[:]))
+
+        scores, negm, p_win, p_plain, z, e = [], [], [], [], [], []
+        for h in range(HALVES):
+            q_bf = sb("q_bf%d" % h, [P, P, PACK], BF16)
+            nc.scalar.copy(q_bf[:], q_raw[h][:].rearrange("p j q -> p q j"))
+            q_codes = sb("q_codes%d" % h, [P, P], U32)
+            q_scales = sb("q_scales%d" % h, [P, P], U8)
+            nc.vector.quantize_mx(
+                out=q_codes[:].bitcast(FP8X4), scales=q_scales[:], in_=q_bf[:].rearrange("p q j -> p (q j)")
+            )
+            a = psum2.tile([P, I], F32, name="row_bank")
+            nc.tensor.matmul_mx(
+                out=a[:], lhsT=q_codes[:].bitcast(FP8X4), lhsT_scale=q_scales[:],
+                rhs=kw[:].bitcast(FP8X4), rhs_scale=ks[:], start=True, stop=True,
+            )
+            scores.append(a)
+        os_t = psum.tile([P, PACK, P], F32, name="os_t")
+        for r in range(PACK):
+            nc.tensor.transpose(os_t[:, r, :], os_col[:, r : r + 1].to_broadcast([P, P]), ident[:])
+
+        for h in range(HALVES):
+            t = sb("negm%d" % h, [P, 1], F32)
+            nc.vector.tensor_reduce(t[:], scores[h][:], axis=AX.X, op=ALU.max, negate=True)
+            negm.append(t)
+        bias = []
+        for h in range(HALVES):
+            pw = sb("p_win%d" % h, [P, I + SPARE], F32)
+            nc.gpsimd.memset(pw[:, I:], 0.0)
+            pp = sb("p_plain%d" % h, [P, I], F32)
+            zz = sb("z%d" % h, [P, 1], F32)
+            ee = sb("e%d" % h, [P, 1], F32)
+            nc.scalar.activation(pw[:, :I], scores[h][:], ACT.Exp, bias=negm[h][:], accum_out=zz[:])
+            nc.scalar.activation(pp[:], scores[h][:], ACT.Exp, bias=negm[h][:])
+            nc.scalar.activation(ee[:], negm[h][:], ACT.Exp)
+            shifted = sb("shifted%d" % h, [P, 1], F32)
+            nc.gpsimd.tensor_scalar(shifted[:], ee[:], BIG, res[h][:], ALU.min, ALU.mult)
+            b = sb("bias%d" % h, [P, 1], F32)
+            nc.gpsimd.tensor_scalar(b[:], shifted[:], TINY, zz[:], ALU.add, ALU.mult)
+            p_win.append(pw)
+            p_plain.append(pp)
+            z.append(zz)
+            bias.append(b)
+
+        v_codes = sb("v_codes", [P, PACK, P], U32)
+        v_scales = sb("v_scales", [P, PACK, P], U8)
+        v_bf, v_grouped = [], []
+
+        def gather_values(j):
+            g = sb("v_bf%d" % j, [P, I], BF16)
+            nc.vector.tensor_copy(g[:], v_pool[j][:].indirect(offs_sb[:]))
+            v_bf.append(g)
+
+        def turn(src, bank, dst):
+            words = src[:].bitcast(F32)
+            for u in range(2):
+                nc.tensor.transpose(bank[:, u * P : (u + 1) * P], words[:, u : I // 2 : 2], ident[:])
+            nc.scalar.copy(
+                dst.bitcast(F32).rearrange("p (c u) -> p c u", u=2),
+                bank[:, : 2 * P].rearrange("p (u c) -> p c u", u=2),
+            )
+
+        def turn_values(j):
+            bank = psum2.tile([P, 2 * P], F32, name="v_bank")
+            g = sb("v_grouped%d" % j, [P, I], BF16)
+            turn(v_bf[j], bank, g[:])
+            v_grouped.append(g)
+
+        def quantize_values(j):
+            nc.vector.quantize_mx(out=v_codes[:, j, :].bitcast(FP8X4), scales=v_scales[:, j, :], in_=v_grouped[j][:])
+
+        gather_values(0)
+        turn_values(0)
+        pair = []
+        for h in range(HALVES):
+            s = sb("pair%d" % h, [P, I], F32)
+            nc.vector.tensor_tensor(s[:], p_win[h][:].indirect(offs2_sb[:]), p_plain[h][:], ALU.add)
+            pair.append(s)
+        root = []
+        for h in range(HALVES):
+            t = sb("root%d" % h, [P, I], F32)
+            nc.scalar.activation(t[:], pair[h][:], ACT.Abs_reciprocal_sqrt, bias=bias[h][:], scale=z[h][:])
+            root.append(t)
+        gather_values(1)
+        turn_values(1)
+        w = []
+        for h in range(HALVES):
+            g = sb("w_root%d" % h, [P, I], F32)
+            nc.vector.tensor_tensor(g[:], p_plain[h][:], root[h][:], ALU.mult)
+            t = sb("w%d" % h, [P, I], F32)
+            nc.scalar.activation(t[:], g[:], ACT.Square)
+            w.append(t)
+        gather_values(2)
+        turn_values(2)
+        w_grouped = sb("w_grouped", [P, HALVES, I], BF16)
+        for h in range(HALVES):
+            t = sb("w_bf%d" % h, [P, I], BF16)
+            nc.vector.tensor_tensor(
+                t[:].rearrange("p (s r) -> p s r", r=PACK),
+                w[h][:].rearrange("p (s r) -> p s r", r=PACK),
+                os_t[:].rearrange("p r s -> p s r"),
+                ALU.mult,
+            )
+            bank = psum2.tile([P, I], F32, name="row_bank")
+            turn(t, bank, w_grouped[:, h, :])
+        gather_values(3)
+        turn_values(3)
+        w_codes = sb("w_codes", [P, Q], U32)
+        w_scales = sb("w_scales", [P, Q], U8)
+        nc.vector.quantize_mx(
+            out=w_codes[:].bitcast(FP8X4), scales=w_scales[:], in_=w_grouped[:].rearrange("p h c -> p (h c)")
+        )
+        for j in range(PACK):
+            quantize_values(j)
+
+        o_bank = [psum.tile([P, PACK, P], F32, name="o_bank%d" % h) for h in range(HALVES)]
+        o_sb = sb("o_sb", [P, PACK, Q], F32)
+        o_view = out_0.rearrange("(p j) q -> p j q", j=PACK)
+
+        def product(j, h):
+            cols = slice(h * P, (h + 1) * P)
+            nc.tensor.matmul_mx(
+                out=o_bank[h][:, j, :], lhsT=v_codes[:, j, :].bitcast(FP8X4), lhsT_scale=v_scales[:, j, :],
+                rhs=w_codes[:, cols].bitcast(FP8X4), rhs_scale=w_scales[:, cols], start=True, stop=True,
+            )
+
+        last = PACK - 1
+        for h in range(HALVES):
+            for j in range(last):
+                product(j, h)
+            nc.scalar.copy(o_sb[:, :last, h * P : (h + 1) * P], o_bank[h][:, :last, :])
+        nc.sync.dma_start(o_view[:, :last, :], o_sb[:, :last, :])
+        for h in range(HALVES):
+            product(last, h)
+        o_codes = sb("o_codes", [P, Q], U32)
+        o_scales = sb("o_scales", [P, Q], U8)
+        o_bf = [sb("o_bf%d" % h, [P, P, PACK], BF16) for h in range(HALVES)]
+        nc.vector.tensor_copy(o_bf[0][:], o_bank[0][:].rearrange("p j q -> p q j"))
+        nc.scalar.copy(o_bf[1][:], o_bank[1][:].rearrange("p j q -> p q j"))
+        for h in range(HALVES):
+            cols = slice(h * P, (h + 1) * P)
+            nc.scalar.copy(o_sb[:, last, cols], o_bank[h][:, last, :])
+            nc.vector.quantize_mx(
+                out=o_codes[:, cols].bitcast(FP8X4), scales=o_scales[:, cols],
+                in_=o_bf[h][:].rearrange("p q j -> p (q j)"),
+            )
+        nc.scalar.dma_start(o_view[:, last, :], o_sb[:, last, :])
+        nc.sync.dma_start(out_1[0].rearrange("p q t -> p (q t)").bitcast(I32), o_codes[:].bitcast(I32))
+        for quad in range(4):
+            queue = nc.sync if quad % 2 == 0 else nc.scalar
+            queue.dma_start(
+                out_2[0, 4 * quad : 4 * quad + 4, :].bitcast(I32),
+                o_scales[32 * quad : 32 * quad + 4, :].bitcast(I32),
+            )

@@ -21,7 +21,7 @@ P = 128
 PACK = 4
 HALVES = Q // P
 SPARE = 16
-BIG = 1e30
+CAP = 64.0
 TINY = 1e-30
 
 
@@ -33,100 +33,106 @@ def tile_attend_neighbourshare_pl_kernel(
         keep = ctx.enter_context(tc.tile_pool(name="keep", bufs=1))
         psum = ctx.enter_context(tc.psum_pool(name="psum", bufs=1))
         psum2 = ctx.enter_context(tc.psum_pool(name="psum2", bufs=2))
+        psum3 = ctx.enter_context(tc.psum_pool(name="psum3", bufs=4))
 
-        def sb(name, shape, dtype):
-            return keep.tile(shape, dtype, name=name, align_bytes=64)
+        def sb(name, shape, dtype, tag=None):
+            return keep.tile(shape, dtype, name=name, tag=tag or name, align_bytes=64)
 
         offs_sb = sb("offs_sb", [P, I // 16], U16)
         offs2_sb = sb("offs2_sb", [P, I // 16], U16)
-        kw_pool = sb("kw_pool", [P, T], I32)
         ks_pool = sb("ks_pool", [P, T], U8)
-        nc.vector.memset(ks_pool[:].bitcast(I32), 0)
+        kw_pool = sb("kw_pool", [P, T], I32)
+        q_raw = [sb("q_raw%d" % h, [P, PACK, P], F32) for h in range(HALVES)]
+        q_view = query.rearrange("(p j) q -> p j q", j=PACK)
+        nc.gpsimd.memset(ks_pool[:].bitcast(I32), 0)
         nc.sync.dma_start(offs_sb[:], offs)
+        nc.sync.dma_start(q_raw[0][:], q_view[:, :, :P])
         for quad in range(4):
-            nc.scalar.dma_start(
+            nc.sync.dma_start(
                 ks_pool[32 * quad : 32 * quad + 4, :].bitcast(I32),
                 keys_scales[0, 4 * quad : 4 * quad + 4, :].bitcast(I32),
             )
         nc.sync.dma_start(kw_pool[:], keys_words[0].rearrange("p n t -> p (n t)").bitcast(I32))
-        q_view = query.rearrange("(p j) q -> p j q", j=PACK)
-        q_raw = []
-        for h in range(HALVES):
-            t = sb("q_raw%d" % h, [P, PACK, P], F32)
-            nc.sync.dma_start(t[:], q_view[:, :, h * P : (h + 1) * P])
-            q_raw.append(t)
-        v_view = vals.rearrange("(p j) t -> p j t", j=PACK)
-        v_pool = [sb("v_pool%d" % j, [P, T], F32) for j in range(PACK)]
-        nc.sync.dma_start(v_pool[0][:], v_view[:, 0, :])
+        nc.sync.dma_start(q_raw[1][:], q_view[:, :, P:])
         nc.sync.dma_start(offs2_sb[:], offs2)
-        os_col = sb("os_col", [P, PACK], F32)
-        nc.sync.dma_start(os_col[:], slot_factor.rearrange("o (s r) -> s (o r)", r=PACK))
-        res = []
-        for h in range(HALVES):
-            t = sb("res%d" % h, [P, 1], F32)
-            nc.sync.dma_start(t[:], reserve[h * P : (h + 1) * P, :])
-            res.append(t)
-        for j in range(1, PACK):
-            nc.sync.dma_start(v_pool[j][:], v_view[:, j, :])
-
+        v_view = vals.rearrange("(p j) t -> p j t", j=PACK)
+        v_pool = []
+        for j in range(PACK):
+            t = sb("v_pool%d" % j, [P, T], F32)
+            nc.sync.dma_start(t[:], v_view[:, j, :])
+            v_pool.append(t)
         ident = sb("ident", [P, P], F32)
         make_identity(nc, ident[:])
+        res = sb("res", [P, HALVES], F32)
+        with nc.allow_non_contiguous_dma(reason="one reserve value per query row"):
+            nc.gpsimd.dma_start(res[:], reserve.rearrange("(h p) o -> p (h o)", p=P))
+        os_col = sb("os_col", [P, PACK], F32)
+        nc.gpsimd.dma_start(os_col[:], slot_factor.rearrange("o (s r) -> s (o r)", r=PACK))
+        p_win = [sb("p_win%d" % h, [P, I + SPARE], F32) for h in range(HALVES)]
+        for h in range(HALVES):
+            nc.scalar.copy(p_win[h][:, I:], ident[:, :SPARE])
 
         ks = sb("ks", [P, I], U8)
         nc.vector.tensor_copy(ks[:], ks_pool[:].indirect(offs_sb[:]))
-        kw = sb("kw", [P, I], U32)
-        nc.vector.tensor_copy(kw[:], kw_pool[:].bitcast(U32).indirect(offs_sb[:]))
+        q_codes = sb("q_codes", [P, Q], U32)
+        q_scales = sb("q_scales", [P, Q], U8)
 
-        scores, negm, p_win, p_plain, z, e = [], [], [], [], [], []
-        for h in range(HALVES):
+        def quantize_queries(h):
+            cols = slice(h * P, (h + 1) * P)
             q_bf = sb("q_bf%d" % h, [P, P, PACK], BF16)
             nc.scalar.copy(q_bf[:], q_raw[h][:].rearrange("p j q -> p q j"))
-            q_codes = sb("q_codes%d" % h, [P, P], U32)
-            q_scales = sb("q_scales%d" % h, [P, P], U8)
             nc.vector.quantize_mx(
-                out=q_codes[:].bitcast(FP8X4), scales=q_scales[:], in_=q_bf[:].rearrange("p q j -> p (q j)")
+                out=q_codes[:, cols].bitcast(FP8X4), scales=q_scales[:, cols],
+                in_=q_bf[:].rearrange("p q j -> p (q j)"),
             )
+
+        quantize_queries(0)
+        kw = sb("kw", [P, I], U32)
+        nc.vector.tensor_copy(kw[:], kw_pool[:].bitcast(U32).indirect(offs_sb[:]))
+        quantize_queries(1)
+
+        scores = []
+        negm = sb("negm", [P, HALVES], F32)
+        for h in range(HALVES):
+            cols = slice(h * P, (h + 1) * P)
             a = psum2.tile([P, I], F32, name="row_bank")
             nc.tensor.matmul_mx(
-                out=a[:], lhsT=q_codes[:].bitcast(FP8X4), lhsT_scale=q_scales[:],
+                out=a[:], lhsT=q_codes[:, cols].bitcast(FP8X4), lhsT_scale=q_scales[:, cols],
                 rhs=kw[:].bitcast(FP8X4), rhs_scale=ks[:], start=True, stop=True,
             )
+            nc.vector.tensor_reduce(negm[:, h : h + 1], a[:], axis=AX.X, op=ALU.max, negate=True)
             scores.append(a)
-        os_t = psum.tile([P, PACK, P], F32, name="os_t")
+        p_plain = [sb("p_plain%d" % h, [P, I], F32) for h in range(HALVES)]
+        z = sb("z", [P, HALVES], F32)
+
+        def exp_window(h):
+            col = slice(h, h + 1)
+            nc.scalar.activation(p_win[h][:, :I], scores[h][:], ACT.Exp, bias=negm[:, col], accum_out=z[:, col])
+
+        def exp_plain(h):
+            nc.scalar.activation(p_plain[h][:], scores[h][:], ACT.Exp, bias=negm[:, h : h + 1])
+
+        exp_window(0)
+        exp_plain(0)
+        lifted = sb("lifted", [P, HALVES], F32)
+        nc.scalar.activation(lifted[:], negm[:], ACT.Relu, scale=-1.0, bias=CAP)
+        exp_window(1)
+        shift = sb("shift", [P, HALVES], F32)
+        nc.scalar.activation(shift[:], lifted[:], ACT.Exp, scale=-1.0, bias=CAP)
+        exp_plain(1)
+        bias = sb("bias", [P, HALVES], F32)
+        for h in range(HALVES):
+            col = slice(h, h + 1)
+            nc.scalar.activation(bias[:, col], shift[:, col], ACT.Identity, scale=res[:, col], bias=TINY)
+        z_root = sb("z_root", [P, HALVES], F32)
+        nc.scalar.activation(z_root[:], z[:], ACT.Abs_reciprocal_sqrt)
+
+        os_t = psum2.tile([P, PACK, P], F32, name="row_bank")
         for r in range(PACK):
             nc.tensor.transpose(os_t[:, r, :], os_col[:, r : r + 1].to_broadcast([P, P]), ident[:])
 
-        for h in range(HALVES):
-            t = sb("negm%d" % h, [P, 1], F32)
-            nc.vector.tensor_reduce(t[:], scores[h][:], axis=AX.X, op=ALU.max, negate=True)
-            negm.append(t)
-        bias = []
-        for h in range(HALVES):
-            pw = sb("p_win%d" % h, [P, I + SPARE], F32)
-            nc.gpsimd.memset(pw[:, I:], 0.0)
-            pp = sb("p_plain%d" % h, [P, I], F32)
-            zz = sb("z%d" % h, [P, 1], F32)
-            ee = sb("e%d" % h, [P, 1], F32)
-            nc.scalar.activation(pw[:, :I], scores[h][:], ACT.Exp, bias=negm[h][:], accum_out=zz[:])
-            nc.scalar.activation(pp[:], scores[h][:], ACT.Exp, bias=negm[h][:])
-            nc.scalar.activation(ee[:], negm[h][:], ACT.Exp)
-            shifted = sb("shifted%d" % h, [P, 1], F32)
-            nc.gpsimd.tensor_scalar(shifted[:], ee[:], BIG, res[h][:], ALU.min, ALU.mult)
-            b = sb("bias%d" % h, [P, 1], F32)
-            nc.gpsimd.tensor_scalar(b[:], shifted[:], TINY, zz[:], ALU.add, ALU.mult)
-            p_win.append(pw)
-            p_plain.append(pp)
-            z.append(zz)
-            bias.append(b)
-
         v_codes = sb("v_codes", [P, PACK, P], U32)
         v_scales = sb("v_scales", [P, PACK, P], U8)
-        v_bf, v_grouped = [], []
-
-        def gather_values(j):
-            g = sb("v_bf%d" % j, [P, I], BF16)
-            nc.vector.tensor_copy(g[:], v_pool[j][:].indirect(offs_sb[:]))
-            v_bf.append(g)
 
         def turn(src, bank, dst):
             words = src[:].bitcast(F32)
@@ -137,58 +143,64 @@ def tile_attend_neighbourshare_pl_kernel(
                 bank[:, : 2 * P].rearrange("p (u c) -> p c u", u=2),
             )
 
-        def turn_values(j):
-            bank = psum2.tile([P, 2 * P], F32, name="v_bank")
-            g = sb("v_grouped%d" % j, [P, I], BF16)
-            turn(v_bf[j], bank, g[:])
-            v_grouped.append(g)
+        def gather_values(j, tag=None):
+            g = sb("v_bf%d" % j, [P, I], BF16, tag)
+            nc.vector.tensor_copy(g[:], v_pool[j][:].indirect(offs_sb[:]))
+            return g
 
-        def quantize_values(j):
-            nc.vector.quantize_mx(out=v_codes[:, j, :].bitcast(FP8X4), scales=v_scales[:, j, :], in_=v_grouped[j][:])
+        def turn_values(g, dst):
+            bank = psum3.tile([P, 2 * P], F32, name="turn_bank")
+            turn(g, bank, dst)
 
-        gather_values(0)
-        turn_values(0)
-        pair = []
-        for h in range(HALVES):
-            s = sb("pair%d" % h, [P, I], F32)
-            nc.vector.tensor_tensor(s[:], p_win[h][:].indirect(offs2_sb[:]), p_plain[h][:], ALU.add)
-            pair.append(s)
+        def quantize_values(first, count, grouped):
+            nc.vector.quantize_mx(
+                out=v_codes[:, first : first + count, :].rearrange("p j c -> p (j c)").bitcast(FP8X4),
+                scales=v_scales[:, first : first + count, :].rearrange("p j c -> p (j c)"),
+                in_=grouped,
+            )
+
+        v_first = sb("v_first", [P, I], BF16)
+        turn_values(gather_values(0), v_first[:])
         root = []
         for h in range(HALVES):
+            pair = sb("pair%d" % h, [P, I], F32, "v_pool0" if h == 0 else None)
+            nc.vector.tensor_tensor(pair[:], p_win[h][:].indirect(offs2_sb[:]), p_plain[h][:], ALU.add)
             t = sb("root%d" % h, [P, I], F32)
-            nc.scalar.activation(t[:], pair[h][:], ACT.Abs_reciprocal_sqrt, bias=bias[h][:], scale=z[h][:])
+            nc.scalar.activation(t[:], pair[:], ACT.Abs_reciprocal_sqrt, bias=bias[:, h : h + 1])
             root.append(t)
-        gather_values(1)
-        turn_values(1)
+        v_bf1 = gather_values(1)
+        quantize_values(0, 1, v_first[:])
         w = []
         for h in range(HALVES):
             g = sb("w_root%d" % h, [P, I], F32)
             nc.vector.tensor_tensor(g[:], p_plain[h][:], root[h][:], ALU.mult)
             t = sb("w%d" % h, [P, I], F32)
-            nc.scalar.activation(t[:], g[:], ACT.Square)
+            nc.scalar.activation(t[:], g[:], ACT.Square, scale=z_root[:, h : h + 1])
             w.append(t)
-        gather_values(2)
-        turn_values(2)
+        v_middle = sb("v_middle", [P, 2, I], BF16, "w_root1")
+        turn_values(v_bf1, v_middle[:, 0, :])
+        turn_values(gather_values(2, "root1"), v_middle[:, 1, :])
         w_grouped = sb("w_grouped", [P, HALVES, I], BF16)
         for h in range(HALVES):
-            t = sb("w_bf%d" % h, [P, I], BF16)
+            t = sb("w_bf%d" % h, [P, I], BF16, "v_pool2" if h == 0 else None)
             nc.vector.tensor_tensor(
                 t[:].rearrange("p (s r) -> p s r", r=PACK),
                 w[h][:].rearrange("p (s r) -> p s r", r=PACK),
                 os_t[:].rearrange("p r s -> p s r"),
                 ALU.mult,
             )
-            bank = psum2.tile([P, I], F32, name="row_bank")
+            bank = psum3.tile([P, 2 * P], F32, name="turn_bank")
             turn(t, bank, w_grouped[:, h, :])
-        gather_values(3)
-        turn_values(3)
-        w_codes = sb("w_codes", [P, Q], U32)
+            w_last = t
+        v_last = sb("v_last", [P, I], BF16)
+        turn_values(gather_values(3, "w1"), v_last[:])
+        quantize_values(1, 2, v_middle[:].rearrange("p j c -> p (j c)"))
+        w_codes = sb("w_codes", [P, Q], U32, "v_pool3")
         w_scales = sb("w_scales", [P, Q], U8)
         nc.vector.quantize_mx(
             out=w_codes[:].bitcast(FP8X4), scales=w_scales[:], in_=w_grouped[:].rearrange("p h c -> p (h c)")
         )
-        for j in range(PACK):
-            quantize_values(j)
+        quantize_values(3, 1, v_last[:])
 
         o_bank = [psum.tile([P, PACK, P], F32, name="o_bank%d" % h) for h in range(HALVES)]
         o_sb = sb("o_sb", [P, PACK, Q], F32)

@@ -48,26 +48,27 @@ def tile_attend_neighbourshare_pl_kernel(
         nc.sync.dma_start(offs_sb[:], offs)
         nc.sync.dma_start(q_raw[0][:], q_view[:, :, :P])
         for quad in range(4):
-            nc.sync.dma_start(
+            queue = nc.sync if quad < 2 else nc.scalar
+            queue.dma_start(
                 ks_pool[32 * quad : 32 * quad + 4, :].bitcast(I32),
                 keys_scales[0, 4 * quad : 4 * quad + 4, :].bitcast(I32),
             )
         nc.sync.dma_start(kw_pool[:], keys_words[0].rearrange("p n t -> p (n t)").bitcast(I32))
         nc.sync.dma_start(q_raw[1][:], q_view[:, :, P:])
-        nc.sync.dma_start(offs2_sb[:], offs2)
         v_view = vals.rearrange("(p j) t -> p j t", j=PACK)
-        v_pool = []
-        for j in range(PACK):
-            t = sb("v_pool%d" % j, [P, T], F32)
-            nc.sync.dma_start(t[:], v_view[:, j, :])
-            v_pool.append(t)
+        v_pool = [sb("v_pool%d" % j, [P, T], F32) for j in range(PACK)]
+        res = sb("res", [P, HALVES], F32)
+        os_col = sb("os_col", [P, PACK], F32)
+        nc.sync.dma_start(os_col[:], slot_factor.rearrange("o (s r) -> s (o r)", r=PACK))
+        nc.sync.dma_start(v_pool[0][:], v_view[:, 0, :])
+        nc.sync.dma_start(offs2_sb[:], offs2)
+        nc.sync.dma_start(v_pool[1][:], v_view[:, 1, :])
+        with nc.allow_non_contiguous_dma(reason="one reserve value per query row"):
+            nc.sync.dma_start(res[:], reserve.rearrange("(h p) o -> p (h o)", p=P))
+        nc.sync.dma_start(v_pool[2][:], v_view[:, 2, :])
+        nc.sync.dma_start(v_pool[3][:], v_view[:, 3, :])
         ident = sb("ident", [P, P], F32)
         make_identity(nc, ident[:])
-        res = sb("res", [P, HALVES], F32)
-        with nc.allow_non_contiguous_dma(reason="one reserve value per query row"):
-            nc.gpsimd.dma_start(res[:], reserve.rearrange("(h p) o -> p (h o)", p=P))
-        os_col = sb("os_col", [P, PACK], F32)
-        nc.gpsimd.dma_start(os_col[:], slot_factor.rearrange("o (s r) -> s (o r)", r=PACK))
         p_win = [sb("p_win%d" % h, [P, I + SPARE], F32) for h in range(HALVES)]
         for h in range(HALVES):
             nc.scalar.copy(p_win[h][:, I:], ident[:, :SPARE])
@@ -120,21 +121,10 @@ def tile_attend_neighbourshare_pl_kernel(
         shift = sb("shift", [P, HALVES], F32)
         nc.scalar.activation(shift[:], lifted[:], ACT.Exp, scale=-1.0, bias=CAP)
         exp_plain(1)
-        bias = sb("bias", [P, HALVES], F32)
-        for h in range(HALVES):
-            col = slice(h, h + 1)
-            nc.scalar.activation(bias[:, col], shift[:, col], ACT.Identity, scale=res[:, col], bias=TINY)
-        z_root = sb("z_root", [P, HALVES], F32)
-        nc.scalar.activation(z_root[:], z[:], ACT.Abs_reciprocal_sqrt)
-
-        os_t = psum2.tile([P, PACK, P], F32, name="row_bank")
-        for r in range(PACK):
-            nc.tensor.transpose(os_t[:, r, :], os_col[:, r : r + 1].to_broadcast([P, P]), ident[:])
-
-        v_codes = sb("v_codes", [P, PACK, P], U32)
         v_scales = sb("v_scales", [P, PACK, P], U8)
 
-        def turn(src, bank, dst):
+        def turn(src, dst):
+            bank = psum3.tile([P, 2 * P], F32, name="turn_bank")
             words = src[:].bitcast(F32)
             for u in range(2):
                 nc.tensor.transpose(bank[:, u * P : (u + 1) * P], words[:, u : I // 2 : 2], ident[:])
@@ -148,10 +138,6 @@ def tile_attend_neighbourshare_pl_kernel(
             nc.vector.tensor_copy(g[:], v_pool[j][:].indirect(offs_sb[:]))
             return g
 
-        def turn_values(g, dst):
-            bank = psum3.tile([P, 2 * P], F32, name="turn_bank")
-            turn(g, bank, dst)
-
         def quantize_values(first, count, grouped):
             nc.vector.quantize_mx(
                 out=v_codes[:, first : first + count, :].rearrange("p j c -> p (j c)").bitcast(FP8X4),
@@ -159,17 +145,28 @@ def tile_attend_neighbourshare_pl_kernel(
                 in_=grouped,
             )
 
-        v_first = sb("v_first", [P, I], BF16)
-        turn_values(gather_values(0), v_first[:])
-        root = []
+        v_bf0 = gather_values(0)
+        bias = sb("bias", [P, HALVES], F32)
         for h in range(HALVES):
-            pair = sb("pair%d" % h, [P, I], F32, "v_pool0" if h == 0 else None)
+            col = slice(h, h + 1)
+            nc.scalar.activation(bias[:, col], shift[:, col], ACT.Identity, scale=res[:, col], bias=TINY)
+        z_root = sb("z_root", [P, HALVES], F32)
+        nc.scalar.activation(z_root[:], z[:], ACT.Abs_reciprocal_sqrt)
+
+        os_t = psum2.tile([P, PACK, P], F32, name="row_bank")
+        for r in range(PACK):
+            nc.tensor.transpose(os_t[:, r, :], os_col[:, r : r + 1].to_broadcast([P, P]), ident[:])
+
+        root = []
+        pairs = []
+        for h in range(HALVES):
+            pair = sb("pair%d" % h, [P, I], F32)
             nc.vector.tensor_tensor(pair[:], p_win[h][:].indirect(offs2_sb[:]), p_plain[h][:], ALU.add)
             t = sb("root%d" % h, [P, I], F32)
             nc.scalar.activation(t[:], pair[:], ACT.Abs_reciprocal_sqrt, bias=bias[:, h : h + 1])
             root.append(t)
+            pairs.append(pair)
         v_bf1 = gather_values(1)
-        quantize_values(0, 1, v_first[:])
         w = []
         for h in range(HALVES):
             g = sb("w_root%d" % h, [P, I], F32)
@@ -177,29 +174,39 @@ def tile_attend_neighbourshare_pl_kernel(
             t = sb("w%d" % h, [P, I], F32)
             nc.scalar.activation(t[:], g[:], ACT.Square, scale=z_root[:, h : h + 1])
             w.append(t)
-        v_middle = sb("v_middle", [P, 2, I], BF16, "w_root1")
-        turn_values(v_bf1, v_middle[:, 0, :])
-        turn_values(gather_values(2, "root1"), v_middle[:, 1, :])
-        w_grouped = sb("w_grouped", [P, HALVES, I], BF16)
+        v_bf2 = gather_values(2, "pair1")
+        w_bf = []
         for h in range(HALVES):
-            t = sb("w_bf%d" % h, [P, I], BF16, "v_pool2" if h == 0 else None)
+            t = sb("w_bf%d" % h, [P, I], BF16)
             nc.vector.tensor_tensor(
                 t[:].rearrange("p (s r) -> p s r", r=PACK),
                 w[h][:].rearrange("p (s r) -> p s r", r=PACK),
                 os_t[:].rearrange("p r s -> p s r"),
                 ALU.mult,
             )
-            bank = psum3.tile([P, 2 * P], F32, name="turn_bank")
-            turn(t, bank, w_grouped[:, h, :])
-            w_last = t
+            w_bf.append(t)
+        v_first = sb("v_first", [P, 2, I], BF16, "w0")
+        turn(v_bf0, v_first[:, 0, :])
+        turn(v_bf1, v_first[:, 1, :])
+        v_third = sb("v_third", [P, I], BF16)
+        turn(v_bf2, v_third[:])
+        w_grouped = [sb("w_grouped%d" % h, [P, I], BF16) for h in range(HALVES)]
+        for h in range(HALVES):
+            turn(w_bf[h], w_grouped[h][:])
         v_last = sb("v_last", [P, I], BF16)
-        turn_values(gather_values(3, "w1"), v_last[:])
-        quantize_values(1, 2, v_middle[:].rearrange("p j c -> p (j c)"))
-        w_codes = sb("w_codes", [P, Q], U32, "v_pool3")
-        w_scales = sb("w_scales", [P, Q], U8)
-        nc.vector.quantize_mx(
-            out=w_codes[:].bitcast(FP8X4), scales=w_scales[:], in_=w_grouped[:].rearrange("p h c -> p (h c)")
-        )
+        turn(gather_values(3, "w_root1"), v_last[:])
+        codes = sb("codes", [P, PACK + HALVES, P], U32, "v_pool3")
+        v_codes = codes[:, :PACK, :]
+        w_codes = [codes[:, PACK + h, :] for h in range(HALVES)]
+        w_scales = [sb("w_scales%d" % h, [P, P], U8) for h in range(HALVES)]
+
+        def quantize_weights(h):
+            nc.vector.quantize_mx(out=w_codes[h].bitcast(FP8X4), scales=w_scales[h][:], in_=w_grouped[h][:])
+
+        quantize_weights(0)
+        quantize_values(0, 2, v_first[:].rearrange("p j c -> p (j c)"))
+        quantize_values(2, 1, v_third[:])
+        quantize_weights(1)
         quantize_values(3, 1, v_last[:])
 
         o_bank = [psum.tile([P, PACK, P], F32, name="o_bank%d" % h) for h in range(HALVES)]
@@ -207,10 +214,9 @@ def tile_attend_neighbourshare_pl_kernel(
         o_view = out_0.rearrange("(p j) q -> p j q", j=PACK)
 
         def product(j, h):
-            cols = slice(h * P, (h + 1) * P)
             nc.tensor.matmul_mx(
                 out=o_bank[h][:, j, :], lhsT=v_codes[:, j, :].bitcast(FP8X4), lhsT_scale=v_scales[:, j, :],
-                rhs=w_codes[:, cols].bitcast(FP8X4), rhs_scale=w_scales[:, cols], start=True, stop=True,
+                rhs=w_codes[h].bitcast(FP8X4), rhs_scale=w_scales[h][:], start=True, stop=True,
             )
 
         last = PACK - 1

from contextlib import ExitStack

import concourse.mybir as mybir
from concourse.masks import make_identity

D, E, T, I, Q = 512, 512, 2048, 512, 256
FLOPS = 2 * D * Q * I + 2 * I * E * Q

F32 = mybir.dt.float32
BF16 = mybir.dt.bfloat16
U32 = mybir.dt.uint32
I32 = mybir.dt.int32
U16 = mybir.dt.uint16
U8 = mybir.dt.uint8
FP8X4 = mybir.dt.float8_e4m3fn_x4
ALU = mybir.AluOpType
ACT = mybir.ActivationFunctionType
AX = mybir.AxisListType

P = 128
PACK = 4
HALVES = Q // P
SPARE = 16
CAP = 64.0
TINY = 1e-30


def tile_attend_neighbourshare_pl_kernel(
    tc, query, keys_words, keys_scales, reserve, slot_factor, vals, offs2, offs, out_0, out_1, out_2
):
    nc = tc.nc
    with ExitStack() as ctx:
        keep = ctx.enter_context(tc.tile_pool(name="keep", bufs=1))
        psum = ctx.enter_context(tc.psum_pool(name="psum", bufs=1))
        psum2 = ctx.enter_context(tc.psum_pool(name="psum2", bufs=2))
        psum3 = ctx.enter_context(tc.psum_pool(name="psum3", bufs=4))

        def sb(name, shape, dtype, tag=None):
            return keep.tile(shape, dtype, name=name, tag=tag or name, align_bytes=64)

        offs_sb = sb("offs_sb", [P, I // 16], U16)
        offs2_sb = sb("offs2_sb", [P, I // 16], U16)
        ks_pool = sb("ks_pool", [P, T], U8)
        kw_pool = sb("kw_pool", [P, T], I32)
        q_raw = [sb("q_raw%d" % h, [P, PACK, P], F32) for h in range(HALVES)]
        q_view = query.rearrange("(p j) q -> p j q", j=PACK)
        nc.gpsimd.memset(ks_pool[:].bitcast(I32), 0)
        nc.sync.dma_start(offs_sb[:], offs)
        nc.sync.dma_start(q_raw[0][:], q_view[:, :, :P])
        for quad in range(4):
            queue = nc.sync if quad < 2 else nc.scalar
            queue.dma_start(
                ks_pool[32 * quad : 32 * quad + 4, :].bitcast(I32),
                keys_scales[0, 4 * quad : 4 * quad + 4, :].bitcast(I32),
            )
        nc.sync.dma_start(kw_pool[:], keys_words[0].rearrange("p n t -> p (n t)").bitcast(I32))
        nc.sync.dma_start(q_raw[1][:], q_view[:, :, P:])
        v_view = vals.rearrange("(p j) t -> p j t", j=PACK)
        v_pool = [sb("v_pool%d" % j, [P, T], F32) for j in range(PACK)]
        res = sb("res", [P, HALVES], F32)
        os_col = sb("os_col", [P, PACK], F32)
        nc.sync.dma_start(os_col[:], slot_factor.rearrange("o (s r) -> s (o r)", r=PACK))
        nc.sync.dma_start(v_pool[0][:], v_view[:, 0, :])
        nc.sync.dma_start(offs2_sb[:], offs2)
        nc.sync.dma_start(v_pool[1][:], v_view[:, 1, :])
        with nc.allow_non_contiguous_dma(reason="one reserve value per query row"):
            nc.sync.dma_start(res[:], reserve.rearrange("(h p) o -> p (h o)", p=P))
        nc.sync.dma_start(v_pool[2][:], v_view[:, 2, :])
        nc.sync.dma_start(v_pool[3][:], v_view[:, 3, :])
        ident = sb("ident", [P, P], F32)
        make_identity(nc, ident[:])
        p_win = [sb("p_win%d" % h, [P, I + SPARE], F32) for h in range(HALVES)]
        for h in range(HALVES):
            nc.scalar.copy(p_win[h][:, I:], ident[:, :SPARE])

        ks = sb("ks", [P, I], U8)
        nc.vector.tensor_copy(ks[:], ks_pool[:].indirect(offs_sb[:]))
        q_codes = sb("q_codes", [P, Q], U32)
        q_scales = sb("q_scales", [P, Q], U8)

        def quantize_queries(h):
            cols = slice(h * P, (h + 1) * P)
            q_bf = sb("q_bf%d" % h, [P, P, PACK], BF16)
            nc.scalar.copy(q_bf[:], q_raw[h][:].rearrange("p j q -> p q j"))
            nc.vector.quantize_mx(
                out=q_codes[:, cols].bitcast(FP8X4), scales=q_scales[:, cols],
                in_=q_bf[:].rearrange("p q j -> p (q j)"),
            )

        quantize_queries(0)
        kw = sb("kw", [P, I], U32)
        nc.vector.tensor_copy(kw[:], kw_pool[:].bitcast(U32).indirect(offs_sb[:]))
        quantize_queries(1)

        scores = []
        negm = sb("negm", [P, HALVES], F32)
        for h in range(HALVES):
            cols = slice(h * P, (h + 1) * P)
            a = psum2.tile([P, I], F32, name="row_bank")
            nc.tensor.matmul_mx(
                out=a[:], lhsT=q_codes[:, cols].bitcast(FP8X4), lhsT_scale=q_scales[:, cols],
                rhs=kw[:].bitcast(FP8X4), rhs_scale=ks[:], start=True, stop=True,
            )
            nc.vector.tensor_reduce(negm[:, h : h + 1], a[:], axis=AX.X, op=ALU.max, negate=True)
            scores.append(a)
        p_plain = [sb("p_plain%d" % h, [P, I], F32) for h in range(HALVES)]
        z = sb("z", [P, HALVES], F32)

        def exp_window(h):
            col = slice(h, h + 1)
            nc.scalar.activation(p_win[h][:, :I], scores[h][:], ACT.Exp, bias=negm[:, col], accum_out=z[:, col])

        def exp_plain(h):
            nc.scalar.activation(p_plain[h][:], scores[h][:], ACT.Exp, bias=negm[:, h : h + 1])

        exp_window(0)
        exp_plain(0)
        lifted = sb("lifted", [P, HALVES], F32)
        nc.scalar.activation(lifted[:], negm[:], ACT.Relu, scale=-1.0, bias=CAP)
        exp_window(1)
        shift = sb("shift", [P, HALVES], F32)
        nc.scalar.activation(shift[:], lifted[:], ACT.Exp, scale=-1.0, bias=CAP)
        exp_plain(1)
        v_scales = sb("v_scales", [P, PACK, P], U8)

        def turn(src, dst):
            bank = psum3.tile([P, 2 * P], F32, name="turn_bank")
            words = src[:].bitcast(F32)
            for u in range(2):
                nc.tensor.transpose(bank[:, u * P : (u + 1) * P], words[:, u : I // 2 : 2], ident[:])
            nc.scalar.copy(
                dst.bitcast(F32).rearrange("p (c u) -> p c u", u=2),
                bank[:, : 2 * P].rearrange("p (u c) -> p c u", u=2),
            )

        def gather_values(j, tag=None):
            g = sb("v_bf%d" % j, [P, I], BF16, tag)
            nc.vector.tensor_copy(g[:], v_pool[j][:].indirect(offs_sb[:]))
            return g

        def quantize_values(first, count, grouped):
            nc.vector.quantize_mx(
                out=v_codes[:, first : first + count, :].rearrange("p j c -> p (j c)").bitcast(FP8X4),
                scales=v_scales[:, first : first + count, :].rearrange("p j c -> p (j c)"),
                in_=grouped,
            )

        v_bf0 = gather_values(0)
        bias = sb("bias", [P, HALVES], F32)
        for h in range(HALVES):
            col = slice(h, h + 1)
            nc.scalar.activation(bias[:, col], shift[:, col], ACT.Identity, scale=res[:, col], bias=TINY)
        z_root = sb("z_root", [P, HALVES], F32)
        nc.scalar.activation(z_root[:], z[:], ACT.Abs_reciprocal_sqrt)

        os_t = psum2.tile([P, PACK, P], F32, name="row_bank")
        for r in range(PACK):
            nc.tensor.transpose(os_t[:, r, :], os_col[:, r : r + 1].to_broadcast([P, P]), ident[:])

        root = []
        pairs = []
        for h in range(HALVES):
            pair = sb("pair%d" % h, [P, I], F32)
            nc.vector.tensor_tensor(pair[:], p_win[h][:].indirect(offs2_sb[:]), p_plain[h][:], ALU.add)
            t = sb("root%d" % h, [P, I], F32)
            nc.scalar.activation(t[:], pair[:], ACT.Abs_reciprocal_sqrt, bias=bias[:, h : h + 1])
            root.append(t)
            pairs.append(pair)
        v_bf1 = gather_values(1)
        w = []
        for h in range(HALVES):
            g = sb("w_root%d" % h, [P, I], F32)
            nc.vector.tensor_tensor(g[:], p_plain[h][:], root[h][:], ALU.mult)
            t = sb("w%d" % h, [P, I], F32)
            nc.scalar.activation(t[:], g[:], ACT.Square, scale=z_root[:, h : h + 1])
            w.append(t)
        v_bf2 = gather_values(2, "pair1")
        w_bf = []
        for h in range(HALVES):
            t = sb("w_bf%d" % h, [P, I], BF16)
            nc.vector.tensor_tensor(
                t[:].rearrange("p (s r) -> p s r", r=PACK),
                w[h][:].rearrange("p (s r) -> p s r", r=PACK),
                os_t[:].rearrange("p r s -> p s r"),
                ALU.mult,
            )
            w_bf.append(t)
        v_first = sb("v_first", [P, 2, I], BF16, "w0")
        turn(v_bf0, v_first[:, 0, :])
        turn(v_bf1, v_first[:, 1, :])
        v_third = sb("v_third", [P, I], BF16)
        turn(v_bf2, v_third[:])
        w_grouped = [sb("w_grouped%d" % h, [P, I], BF16) for h in range(HALVES)]
        for h in range(HALVES):
            turn(w_bf[h], w_grouped[h][:])
        v_last = sb("v_last", [P, I], BF16)
        turn(gather_values(3, "w_root1"), v_last[:])
        codes = sb("codes", [P, PACK + HALVES, P], U32, "v_pool3")
        v_codes = codes[:, :PACK, :]
        w_codes = [codes[:, PACK + h, :] for h in range(HALVES)]
        w_scales = [sb("w_scales%d" % h, [P, P], U8) for h in range(HALVES)]

        def quantize_weights(h):
            nc.vector.quantize_mx(out=w_codes[h].bitcast(FP8X4), scales=w_scales[h][:], in_=w_grouped[h][:])

        quantize_weights(0)
        quantize_values(0, 2, v_first[:].rearrange("p j c -> p (j c)"))
        quantize_values(2, 1, v_third[:])
        quantize_weights(1)
        quantize_values(3, 1, v_last[:])

        o_bank = [psum.tile([P, PACK, P], F32, name="o_bank%d" % h) for h in range(HALVES)]
        o_sb = sb("o_sb", [P, PACK, Q], F32)
        o_view = out_0.rearrange("(p j) q -> p j q", j=PACK)

        def product(j, h):
            nc.tensor.matmul_mx(
                out=o_bank[h][:, j, :], lhsT=v_codes[:, j, :].bitcast(FP8X4), lhsT_scale=v_scales[:, j, :],
                rhs=w_codes[h].bitcast(FP8X4), rhs_scale=w_scales[h][:], start=True, stop=True,
            )

        last = PACK - 1
        for h in range(HALVES):
            for j in range(last):
                product(j, h)
            nc.scalar.copy(o_sb[:, :last, h * P : (h + 1) * P], o_bank[h][:, :last, :])
        nc.sync.dma_start(o_view[:, :last, :], o_sb[:, :last, :])
        for h in range(HALVES):
            product(last, h)
        o_codes = sb("o_codes", [P, Q], U32)
        o_scales = sb("o_scales", [P, Q], U8)
        o_bf = [sb("o_bf%d" % h, [P, P, PACK], BF16) for h in range(HALVES)]
        nc.vector.tensor_copy(o_bf[0][:], o_bank[0][:].rearrange("p j q -> p q j"))
        nc.scalar.copy(o_bf[1][:], o_bank[1][:].rearrange("p j q -> p q j"))
        for h in range(HALVES):
            cols = slice(h * P, (h + 1) * P)
            nc.scalar.copy(o_sb[:, last, cols], o_bank[h][:, last, :])
            nc.vector.quantize_mx(
                out=o_codes[:, cols].bitcast(FP8X4), scales=o_scales[:, cols],
                in_=o_bf[h][:].rearrange("p q j -> p (q j)"),
            )
        nc.scalar.dma_start(o_view[:, last, :], o_sb[:, last, :])
        nc.sync.dma_start(out_1[0].rearrange("p q t -> p (q t)").bitcast(I32), o_codes[:].bitcast(I32))
        for quad in range(4):
            queue = nc.sync if quad % 2 == 0 else nc.scalar
            queue.dma_start(
                out_2[0, 4 * quad : 4 * quad + 4, :].bitcast(I32),
                o_scales[32 * quad : 32 * quad + 4, :].bitcast(I32),
            )
